import numpy as np
import ml_dtypes


def mxq(x, axis, fmt="e4m3"):
    dtype, down = {"e4m3": (ml_dtypes.float8_e4m3fn, 7), "e5m2": (ml_dtypes.float8_e5m2, 14)}[fmt]
    v = np.moveaxis(np.asarray(x, np.float32).astype(ml_dtypes.bfloat16).astype(np.float64), axis, -1)
    blocks = v.reshape(v.shape[:-1] + (-1, 32))
    amax = np.abs(blocks).max(-1, keepdims=True)
    byte = np.maximum(np.where(amax > 0, np.frexp(amax)[1] - 1 + 127, 0) - down, 1)
    scale = np.exp2(byte - 127.0)
    codes = (blocks / scale).astype(np.float32).astype(dtype).astype(np.float64)
    return np.moveaxis((codes * scale).reshape(v.shape), -1, axis)


WIDE = False


def mx_kscale(k):
    if not WIDE:
        return np.ones(k)
    levels = np.array([10, -10, 5, -5, 0])
    if k % 512:
        return np.exp2(np.random.permutation(np.resize(levels, k // 32))).repeat(32)
    a = np.empty((k // 512, 16))
    for p in range(k // 512):
        a[p, :8] = np.random.permutation(np.resize(levels, 8))
        for g in range(8):
            far = levels[np.abs(levels - a[p, g]) >= 10]
            a[p, g + 8] = far[np.random.randint(len(far))]
    return np.exp2(a.ravel()).repeat(32)


def f64(x):
    return np.asarray(x).astype(np.float64)


def striped(idx):
    return np.tile(idx.reshape(-1, 16).T, (8, 1)).astype(np.uint16)


def unstriped(offs):
    return offs[:16].T.reshape(-1).astype(np.int64)


def striped8(idx):
    return np.concatenate([x.reshape(-1, 16).T for x in idx]).astype(np.uint16)


def runs(offs, k):
    lists = np.stack([offs[16 * r : 16 * r + 16].T.reshape(-1) for r in range(8)]).astype(np.int64)
    return lists[np.arange(k) % 512 // 64]


def pack_weight(w):
    k, n = w.shape
    w = f64(np.asarray(w, np.float32).astype(ml_dtypes.bfloat16)).reshape(k // 32, 32, n)
    amax = np.abs(w).max(1)
    byte = np.clip(np.where(amax > 0, np.frexp(amax)[1] - 1 + 127 - 7, 1), 1, 254)
    scaled = (w * np.exp2(127.0 - byte)[:, None, :]).reshape(k, n).astype(np.float32)
    words = np.ascontiguousarray(scaled.reshape(k // 512, 128, 4, n).transpose(0, 1, 3, 2)).astype(ml_dtypes.float8_e4m3fn).view(np.uint8)
    return words, np.ascontiguousarray(byte.astype(np.uint8).reshape(k // 512, 16, n))


def unpack_weight(words, scales):
    g, p, n, _ = words.shape
    vals = np.ascontiguousarray(words).view(ml_dtypes.float8_e4m3fn).astype(np.float64) * np.repeat(np.exp2(scales.astype(np.float64) - 127.0), 8, axis=1)[..., None]
    return vals.transpose(0, 1, 3, 2).reshape(g * 512, n)


E2M1 = np.array([0.0, 0.5, 1.0, 1.5, 2.0, 3.0, 4.0, 6.0, -0.0, -0.5, -1.0, -1.5, -2.0, -3.0, -4.0, -6.0])


def pack_fp4(w):
    k, n = w.shape
    w = f64(np.asarray(w, np.float32).astype(ml_dtypes.bfloat16)).reshape(k // 32, 32, n)
    amax = np.abs(w).max(1)
    mant, ex = np.frexp(amax / 6.0)
    byte = np.clip(np.where(amax > 0, np.where(mant > 0.5, ex, ex - 1) + 127, 1), 1, 254)
    scaled = (w * np.exp2(127.0 - byte)[:, None, :]).reshape(k, n).astype(np.float32)
    c = np.ascontiguousarray(scaled.reshape(k // 512, 128, 4, n).transpose(0, 1, 3, 2)).astype(ml_dtypes.float4_e2m1fn).view(np.uint8) & 0xF
    words = (c[..., 0::2] | (c[..., 1::2] << 4)).reshape(k // 512, 128, 2 * n)
    return np.ascontiguousarray(words), np.ascontiguousarray(byte.astype(np.uint8).reshape(k // 512, 16, n))


def unpack_fp4(words, scales):
    g, _, n = scales.shape
    words = np.ascontiguousarray(words).reshape(g, 128, n, 2)
    nib = np.empty((g, 128, n, 4), np.uint8)
    nib[..., 0::2] = words & 0xF
    nib[..., 1::2] = words >> 4
    vals = E2M1[nib] * np.repeat(np.exp2(scales.astype(np.float64) - 127.0), 8, axis=1)[..., None]
    return vals.transpose(0, 1, 3, 2).reshape(g * 512, n)


def sigmoid(v):
    return 1.0 / (1.0 + np.exp(-np.maximum(v, -700.0)))

def planes(y):
    n, m = y.shape
    v = y.astype(np.float32).astype(ml_dtypes.bfloat16).astype(np.float64).reshape(n // 32, 32, m)
    top = np.abs(v).max(1)
    byte = np.clip(np.where(top > 0, np.frexp(top)[1] - 1 + 127 - 7, 1), 1, 254)
    codes = (v * np.exp2(127.0 - byte)[:, None, :]).reshape(n, m).astype(np.float32).astype(ml_dtypes.float8_e4m3fn).view(np.uint8)
    words = codes.reshape(n // 512, 128, 4, m).transpose(0, 1, 3, 2)
    return np.ascontiguousarray(words), np.ascontiguousarray(byte.astype(np.uint8).reshape(n // 512, 16, m))


K, T, S, N, H, G, W = 512, 1024, 512, 512, 512, 2048, 384


def setup_inputs():
    n = np.random.standard_normal
    s = mx_kscale(K)[:, None]
    u = mx_kscale(S)
    packed_xT = pack_weight(n((K, T)) * s)
    packed_w1 = pack_fp4(n((K, H)) / np.sqrt(K) / s)
    packed_dT = pack_weight(n((K, G)) / s)
    packed_w2 = pack_fp4(n((H, N)) / np.sqrt(2 * H) / u[:, None])
    packed_w3 = pack_fp4(n((H, N)) / np.sqrt(2 * H) / u[:, None])
    return {
        "x_words": packed_xT[0],
        "x_scales": packed_xT[1],
        "w1_words": packed_w1[0],
        "w1_scales": packed_w1[1],
        "d_words": packed_dT[0],
        "d_scales": packed_dT[1],
        "gn": (np.random.uniform(0.5, 1.5, (H, 1)) * u[:, None]).astype(np.float32),
        "gk": (np.random.uniform(0.5, 1.5, (H, 1)) * u[:, None]).astype(np.float32),
        "w2_words": packed_w2[0],
        "w2_scales": packed_w2[1],
        "w3_words": packed_w3[0],
        "w3_scales": packed_w3[1],
        "sl": np.random.uniform(1.5, 3.0, (N, 1)).astype(np.float32),
        "th": (0.5 * n((N, 1))).astype(np.float32),
        "offs": striped(np.random.permutation(T)[:S]),
        "kidx": striped8(np.random.randint(0, G, (8, H))),
        "two": striped(np.random.permutation(T)[:S]),
        "n1": striped(np.random.permutation(S)),
        "n2": striped(np.random.permutation(S)),
        "n3": striped(np.random.permutation(S)[:W]),
        "n4": striped(np.random.permutation(S)[:W]),
        "n5": striped(np.random.permutation(S)),
        "n6": striped(np.random.permutation(S)),
    }


def reference(x_words, x_scales, w1_words, w1_scales, d_words, d_scales, gn, gk, w2_words, w2_scales, w3_words, w3_scales, sl, th, offs, kidx, two, n1, n2, n3, n4, n5, n6):
    xq = unpack_weight(x_words, x_scales)[:, unstriped(offs)]
    y = unpack_fp4(w1_words, w1_scales).T @ xq
    z = f64(gn) * (np.maximum(y[:, unstriped(n1)], y[:, unstriped(n2)]) - (0.75 * y))
    d_kidx = unpack_weight(d_words, d_scales)[np.arange(K)[:, None], runs(kidx, K)]
    x_two = unpack_weight(x_words, x_scales)[:, unstriped(two)]
    s = 0.0625 * (d_kidx.T @ x_two)
    old = s[:, unstriped(n3)]
    pa = s[:, unstriped(n4)]
    ra = old / (np.abs(pa) + 0.5)
    ds = s.copy()
    ds[:, unstriped(n3)] = ra
    z2 = f64(gk) * ds
    h = unpack_fp4(w2_words, w2_scales).T @ mxq(z, 0, "e4m3") + unpack_fp4(w3_words, w3_scales).T @ mxq(z2, 0, "e4m3")
    sg = sigmoid(f64(sl) * (h[:, unstriped(n5)] - f64(th)))
    out_0 = 1.5 * (h * (sg - sg[:, unstriped(n6)]))
    return (out_0,) + planes(out_0)

@@ -1,0 +1,325 @@
+from contextlib import ExitStack
+
+import concourse.mybir as mybir
+
+F32 = mybir.dt.float32
+BF16 = mybir.dt.bfloat16
+I32 = mybir.dt.int32
+U32 = mybir.dt.uint32
+U16 = mybir.dt.uint16
+U8 = mybir.dt.uint8
+FP8X4 = mybir.dt.float8_e4m3fn_x4
+FP4X4 = mybir.dt.float4_e2m1fn_x4
+ACT = mybir.ActivationFunctionType
+ALU = mybir.AluOpType
+
+P = 128
+PACK = 4
+QUADS = 4
+COLS = 512
+HALF = COLS // 2
+TOKENS = 1024
+CODEWORDS = 2048
+SCATTERED = 384
+PER_COLUMN = 16
+ODD_RUN_SHIFT = 14
+
+PAD = 16
+
+FLOPS = 4 * 2 * 512 * 512 * 512
+
+
+def tile_picked_jkeyoverknormedb_none_po_kernel(
+    tc, x_words, x_scales, w1_words, w1_scales, d_words, d_scales, gn, gk,
+    w2_words, w2_scales, w3_words, w3_scales, sl, th,
+    offs, kidx, two, n1, n2, n3, n4, n5, n6, out_0, out_1, out_2,
+):
+    nc = tc.nc
+    with ExitStack() as ctx:
+        sb = ctx.enter_context(tc.tile_pool(name="sb", bufs=1))
+        ps = ctx.enter_context(tc.psum_pool(name="ps", bufs=1))
+
+        def sbuf(name, width, dtype, tag=None):
+            return sb.tile([P, width], dtype, name=name, tag=tag or name, align_bytes=64)
+
+        def bank(name, number, width):
+            return ps.tile([P, width], F32, name=name, tag="bank%d" % number)
+
+        def load_list(name, src):
+            dst = sb.tile([P, src.shape[1]], U16, name=name, tag=name)
+            nc.sync.dma_start(dst[:], src)
+            return dst
+
+        def load_column(name, src):
+            dst = sbuf(name, PACK, F32)
+            nc.gpsimd.dma_start(out=dst[:], in_=src.rearrange("(p t) one -> p (t one)", t=PACK))
+            return dst
+
+        def load_scale_rows(dst, src, first):
+            for q in range(QUADS):
+                nc.sync.dma_start(
+                    out=dst[32 * q + first : 32 * q + first + 4, :].bitcast(I32),
+                    in_=src[0, 4 * q : 4 * q + 4, :].bitcast(I32),
+                )
+
+        def zeroed_plane(name, width, tag=None):
+            plane = sbuf(name, width, U8, tag)
+            nc.vector.memset(plane[:].bitcast(I32), 0)
+            return plane
+
+        def load_fp4_words(name, src, tag=None):
+            dst = sbuf(name, 2 * COLS, U8, tag)
+            nc.sync.dma_start(out=dst[:].bitcast(I32), in_=src[0].bitcast(I32))
+            return dst
+
+        def deal_fp4_words(dealt, raw):
+            nc.scalar.copy(
+                out=dealt[:].bitcast(U16).rearrange("p (t m) -> p t m", t=PACK),
+                in_=raw[:].bitcast(U16).rearrange("p (m t) -> p t m", t=PACK),
+            )
+            return dealt
+
+        def deal_scale_bytes(name, raw, count):
+            dealt = sbuf(name, count * COLS, U8)
+            nc.vector.tensor_copy(
+                out=dealt[:].rearrange("p (w t m) -> p w t m", w=count, t=PACK),
+                in_=raw[:].rearrange("p (w m t) -> p w t m", w=count, t=PACK),
+            )
+            return dealt
+
+        def entries(offsets, start, stop):
+            return offsets[:, start // PER_COLUMN : stop // PER_COLUMN]
+
+        def interleave(copy, name, rows, start, stop):
+            grouped = sbuf(name, PACK * (stop - start), BF16)
+            copy(
+                out=grouped[:].rearrange("p (c i t) -> p c t i", i=4, t=PACK),
+                in_=rows[:, :, start:stop].rearrange("p t (c i) -> p c t i", i=4),
+            )
+            return grouped
+
+        def quantize(name, grouped, width):
+            codes = sbuf(name + "_codes", width, U32)
+            scales = sbuf(name + "_scales", width, U8)
+            nc.vector.quantize_mx(out=codes[:].bitcast(FP8X4), scales=scales[:], in_=grouped[:])
+            return codes, scales
+
+        halves = [(0, HALF), (HALF, COLS)]
+
+        xs_table = zeroed_plane("xs_table", TOKENS)
+        w1s_raw = zeroed_plane("w1s_raw", COLS)
+        ds_table = zeroed_plane("ds_table", CODEWORDS)
+        key_scales = zeroed_plane("key_scales", COLS)
+        minus_one = sbuf("minus_one", 1, F32)
+        nc.vector.memset(minus_one[:], -1.0)
+
+        offs_sb = load_list("offs_sb", offs)
+        xw_table = sbuf("xw_table", TOKENS, I32)
+        nc.sync.dma_start(out=xw_table[:], in_=x_words[0].rearrange("p n t -> p (n t)").bitcast(I32))
+        load_scale_rows(xs_table, x_scales, 0)
+        w1_raw = load_fp4_words("w1_raw", w1_words)
+        kidx_sb = load_list("kidx_sb", kidx)
+        load_scale_rows(w1s_raw, w1_scales, 0)
+        load_scale_rows(ds_table, d_scales, ODD_RUN_SHIFT)
+        two_sb = load_list("two_sb", two)
+        n1_sb = load_list("n1_sb", n1)
+        n2_sb = load_list("n2_sb", n2)
+        n3_sb = load_list("n3_sb", n3)
+        dw_table = sbuf("dw_table", CODEWORDS, I32)
+        nc.sync.dma_start(out=dw_table[:], in_=d_words[0].rearrange("p n t -> p (n t)").bitcast(I32))
+        gn_sb = load_column("gn_sb", gn)
+        n4_sb = load_list("n4_sb", n4)
+        w23_raw = sbuf("w23_raw", 4 * COLS, U8)
+        nc.gpsimd.dma_start(out=w23_raw[:, 0 : 2 * COLS].bitcast(I32), in_=w2_words[0].bitcast(I32))
+        nc.gpsimd.dma_start(out=w23_raw[:, 2 * COLS : 4 * COLS].bitcast(I32), in_=w3_words[0].bitcast(I32))
+        gk_sb = load_column("gk_sb", gk)
+        n5_sb = load_list("n5_sb", n5)
+        n6_sb = load_list("n6_sb", n6)
+        sl_sb = load_column("sl_sb", sl)
+        th_sb = load_column("th_sb", th)
+
+        w1 = deal_fp4_words(sbuf("w1", 2 * COLS, U8), w1_raw)
+        w1s = deal_scale_bytes("w1s", w1s_raw, 1)
+        xq_codes = sbuf("xq_codes", COLS, U32)
+        nc.vector.tensor_copy(xq_codes[:], xw_table[:].bitcast(U32).indirect(offs_sb[:]))
+        xq_scales = sbuf("xq_scales", COLS, U8)
+        nc.vector.tensor_copy(xq_scales[:], xs_table[:].indirect(offs_sb[:]))
+
+        def fp4_pass(acc, words, scales, first, t, codes, code_scales, start, stop):
+            nc.tensor.matmul_mx(
+                out=acc[:],
+                lhsT=words[:, 2 * P * t : 2 * P * (t + 1)].bitcast(FP4X4),
+                lhsT_scale=scales[:, first + P * t : first + P * (t + 1)],
+                rhs=codes[:].bitcast(FP8X4),
+                rhs_scale=code_scales[:],
+                start=start,
+                stop=stop,
+            )
+
+        y = []
+        for t in range(PACK):
+            acc = bank("y_acc%d" % t, t, COLS)
+            fp4_pass(acc, w1, w1s, 0, t, xq_codes, xq_scales, True, True)
+            y_t = sbuf("y%d" % t, COLS + PAD, F32)
+            nc.vector.memset(y_t[:, COLS:], 0.0)
+            nc.scalar.copy(out=y_t[:, :COLS], in_=acc[:])
+            y.append(y_t)
+
+        key_scales_picked = sbuf("key_scales_picked", COLS, U8, "late_scales")
+        nc.vector.tensor_copy(key_scales_picked[:], ds_table[:].indirect(kidx_sb[:]))
+        key_scales_dealt = deal_scale_bytes("key_scales_dealt", key_scales_picked, 1)
+        for q in range(QUADS):
+            nc.sync.dma_start(
+                out=key_scales[32 * q : 32 * q + 4, :].bitcast(I32),
+                in_=key_scales_dealt[32 * q + ODD_RUN_SHIFT : 32 * q + ODD_RUN_SHIFT + 4, :].bitcast(I32),
+            )
+        x2_codes = sbuf("x2_codes", COLS, U32)
+        nc.vector.tensor_copy(x2_codes[:], xw_table[:].bitcast(U32).indirect(two_sb[:]))
+        x2_scales = sbuf("x2_scales", COLS, U8)
+        nc.vector.tensor_copy(x2_scales[:], xs_table[:].indirect(two_sb[:]))
+        key_codes_picked = sbuf("key_codes_picked", COLS, U32)
+        nc.vector.tensor_copy(key_codes_picked[:], dw_table[:].bitcast(U32).indirect(kidx_sb[:]))
+        key_codes = sbuf("key_codes", COLS, U32)
+        nc.vector.tensor_copy(
+            out=key_codes[:].rearrange("p (t m) -> p m t", t=PACK),
+            in_=key_codes_picked[:].rearrange("p (m t) -> p m t", t=PACK),
+        )
+
+        w23s_raw = zeroed_plane("w23s_raw", 2 * COLS, "late_scales")
+        load_scale_rows(w23s_raw[:, 0:COLS], w2_scales, 0)
+        load_scale_rows(w23s_raw[:, COLS : 2 * COLS], w3_scales, 0)
+
+        ds, size = [], []
+        for t in range(PACK):
+            acc = bank("s_acc%d" % t, PACK + t, COLS)
+            nc.tensor.matmul_mx(
+                out=acc[:],
+                lhsT=key_codes[:, P * t : P * (t + 1)].bitcast(FP8X4),
+                lhsT_scale=key_scales[:, P * t : P * (t + 1)],
+                rhs=x2_codes[:].bitcast(FP8X4),
+                rhs_scale=x2_scales[:],
+                start=True,
+                stop=True,
+            )
+            size_t = sbuf("den%d" % t, 2 * COLS, F32)
+            nc.scalar.activation(size_t[:, COLS:], acc[:], ACT.Abs, scale=0.0625)
+            ds_t = sbuf("ds%d" % t, COLS, F32)
+            nc.vector.tensor_scalar(ds_t[:], acc[:], 0.0625, None, ALU.mult)
+            size.append(size_t)
+            ds.append(ds_t)
+
+        old, sg = [], []
+        for t in range(PACK):
+            sg_t = sbuf("sg%d" % t, COLS + SCATTERED, F32)
+            nc.vector.tensor_copy(sg_t[:, COLS:], ds[t][:].indirect(n3_sb[:]))
+            old.append(sg_t[:, COLS:])
+            sg.append(sg_t)
+
+        half_tile = sbuf("half_tile", 1, F32)
+        nc.vector.memset(half_tile[:], 0.5)
+        for t in range(PACK):
+            nc.scalar.activation(size[t][:, :COLS], size[t][:, COLS:], ACT.Ln, bias=half_tile[:])
+
+        inv_den = []
+        for t in range(PACK):
+            inv_t = sbuf("inv_den%d" % t, SCATTERED, F32)
+            nc.scalar.activation(inv_t[:], size[t][:].indirect(n4_sb[:]), ACT.Exp, scale=minus_one[:])
+            inv_den.append(inv_t)
+
+        z2_rows = sb.tile([P, PACK, COLS], BF16, name="z2_rows", align_bytes=64)
+        last = PACK - 1
+        for t in range(last):
+            nc.vector.tensor_tensor(ds[t][:].indirect(n3_sb[:]), old[t], inv_den[t][:], ALU.mult)
+            nc.vector.tensor_scalar(z2_rows[:, t, :], ds[t][:], gk_sb[:, t : t + 1], None, ALU.mult)
+        ratio = sbuf("ratio", SCATTERED, F32)
+        nc.vector.tensor_tensor(ratio[:], old[last], inv_den[last][:], ALU.mult)
+
+        w23 = sbuf("w23", 4 * COLS, U8)
+        w3 = deal_fp4_words(w23[:, 2 * COLS : 4 * COLS], w23_raw[:, 2 * COLS : 4 * COLS])
+        w2 = deal_fp4_words(w23[:, 0 : 2 * COLS], w23_raw[:, 0 : 2 * COLS])
+        w23s = deal_scale_bytes("w23s", w23s_raw, 2)
+
+        y_terms = sb.tile([P, 2 * PACK, COLS], F32, name="y_terms", tag="key_codes_picked", align_bytes=64)
+        for t in range(PACK):
+            nc.vector.tensor_scalar(y_terms[:, t, :], y[t][:, :COLS], gn_sb[:, t : t + 1], -0.75, ALU.mult, ALU.mult)
+
+        h = [sbuf("h%d" % t, 2 * COLS, F32, (None, None, "den1", "den2")[t]) for t in range(PACK)]
+        second_early = sbuf("second_early", COLS, F32)
+        second_late = sb.tile([P, PACK - 1, COLS], F32, name="second_late", tag="den0", align_bytes=64)
+        z_rows = sb.tile([P, PACK, COLS], BF16, name="z_rows", align_bytes=64)
+
+        def z_piece(t, start, stop):
+            first = h[t][:, COLS + start : COLS + stop]
+            second = second_early[:, start:stop] if t == 0 else second_late[:, t - 1, start:stop]
+            larger = y_terms[:, PACK + t, start:stop]
+            nc.scalar.activation(first, y[t][:].indirect(entries(n1_sb, start, stop)), ACT.Copy)
+            nc.scalar.activation(second, y[t][:].indirect(entries(n2_sb, start, stop)), ACT.Copy)
+            nc.vector.tensor_tensor(larger, first, second, ALU.max)
+            nc.vector.scalar_tensor_tensor(
+                z_rows[:, t, start:stop], larger, gn_sb[:, t : t + 1], y_terms[:, t, start:stop], ALU.mult, ALU.add
+            )
+
+        for t in range(PACK):
+            z_piece(t, 0, COLS)
+        nc.scalar.activation(ds[last][:].indirect(n3_sb[:]), ratio[:], ACT.Copy)
+        nc.scalar.activation(z2_rows[:, last, :], ds[last][:], ACT.Copy, scale=gk_sb[:, last : last + 1])
+
+        z_mx, z2_mx = [], []
+        for half, (start, stop) in enumerate(halves):
+            grouped = interleave(nc.vector.tensor_copy, "z_grouped%d" % half, z_rows, start, stop)
+            z_mx.append(quantize("z_%d" % half, grouped, HALF))
+        for half, (start, stop) in enumerate(halves):
+            grouped = interleave(nc.scalar.copy, "z2_grouped%d" % half, z2_rows, start, stop)
+            z2_mx.append(quantize("z2_%d" % half, grouped, HALF))
+        for t in range(PACK):
+            accs = [bank("h_acc%d_%d" % (half, t), PACK * half + t, HALF) for half in range(2)]
+            for half in range(2):
+                fp4_pass(accs[half], w2, w23s, 0, t, *z_mx[half], True, False)
+            for half, (start, stop) in enumerate(halves):
+                fp4_pass(accs[half], w3, w23s, COLS, t, *z2_mx[half], False, True)
+                nc.vector.tensor_copy(out=h[t][:, start:stop], in_=accs[half][:])
+
+        bias = sbuf("bias", PACK, F32)
+        nc.vector.scalar_tensor_tensor(bias[:], sl_sb[:], -1.0, th_sb[:], ALU.mult, ALU.mult)
+        for t in range(PACK):
+            nc.scalar.activation(
+                sg[t][:, :COLS], h[t][:].indirect(n5_sb[:]), ACT.Sigmoid,
+                bias=bias[:, t : t + 1], scale=sl_sb[:, t : t + 1],
+            )
+
+        out_rows = out_0.rearrange("(p t) c -> p t c", t=PACK)
+        out_words = out_1[0].rearrange("p c r -> p (c r)").bitcast(I32)
+        result = sb.tile([P, PACK, COLS], F32, name="result", align_bytes=64)
+
+        def out_piece(t, start, stop):
+            label = "%d_%d" % (t, start)
+            other = sbuf("other" + label, stop - start, F32)
+            looked_up = sg[t][:].indirect(entries(n6_sb, start, stop))
+            if t < 2:
+                nc.vector.tensor_copy(other[:], looked_up)
+            else:
+                nc.scalar.activation(other[:], looked_up, ACT.Copy)
+            gap = sbuf("gap" + label, stop - start, F32)
+            nc.vector.tensor_tensor(gap[:], sg[t][:, start:stop], other[:], ALU.subtract)
+            nc.vector.scalar_tensor_tensor(result[:, t, start:stop], gap[:], 1.5, h[t][:, start:stop], ALU.mult, ALU.mult)
+            nc.sync.dma_start(out=out_rows[:, t, start:stop], in_=result[:, t, start:stop])
+
+        for t in range(PACK - 1):
+            out_piece(t, 0, COLS)
+        out_codes = sbuf("out_codes", COLS, U32)
+        out_scales = sbuf("out_scales", COLS, U8)
+        grouped = []
+        for half, (start, stop) in enumerate(halves):
+            out_piece(PACK - 1, start, stop)
+            copy = nc.scalar.copy if half == 0 else nc.vector.tensor_copy
+            grouped.append(interleave(copy, "out_grouped%d" % half, result, start, stop))
+        for half, (start, stop) in enumerate(halves):
+            nc.vector.quantize_mx(
+                out=out_codes[:, start:stop].bitcast(FP8X4), scales=out_scales[:, start:stop], in_=grouped[half][:]
+            )
+        nc.sync.dma_start(out=out_words, in_=out_codes[:].bitcast(I32))
+        for q in range(QUADS):
+            nc.sync.dma_start(
+                out=out_2[0, 4 * q : 4 * q + 4, :].bitcast(I32),
+                in_=out_scales[32 * q : 32 * q + 4, :].bitcast(I32),
+            )

@@ -90,8 +90,8 @@ def tile_picked_jkeyoverknormedb_none_po_kernel(
         def entries(offsets, start, stop):
             return offsets[:, start // PER_COLUMN : stop // PER_COLUMN]
 
-        def interleave(copy, name, rows, start, stop):
-            grouped = sbuf(name, PACK * (stop - start), BF16)
+        def interleave(copy, name, rows, start, stop, tag=None):
+            grouped = sbuf(name, PACK * (stop - start), BF16, tag)
             copy(
                 out=grouped[:].rearrange("p (c i t) -> p c t i", i=4, t=PACK),
                 in_=rows[:, :, start:stop].rearrange("p t (c i) -> p c t i", i=4),
@@ -110,6 +110,8 @@ def tile_picked_jkeyoverknormedb_none_po_kernel(
         w1s_raw = zeroed_plane("w1s_raw", COLS)
         ds_table = zeroed_plane("ds_table", CODEWORDS)
         key_scales = zeroed_plane("key_scales", COLS)
+        half_tile = sbuf("half_tile", 1, F32)
+        nc.vector.memset(half_tile[:], 0.5)
         minus_one = sbuf("minus_one", 1, F32)
         nc.vector.memset(minus_one[:], -1.0)
 
@@ -127,11 +129,11 @@ def tile_picked_jkeyoverknormedb_none_po_kernel(
         n3_sb = load_list("n3_sb", n3)
         dw_table = sbuf("dw_table", CODEWORDS, I32)
         nc.sync.dma_start(out=dw_table[:], in_=d_words[0].rearrange("p n t -> p (n t)").bitcast(I32))
-        gn_sb = load_column("gn_sb", gn)
         n4_sb = load_list("n4_sb", n4)
         w23_raw = sbuf("w23_raw", 4 * COLS, U8)
         nc.gpsimd.dma_start(out=w23_raw[:, 0 : 2 * COLS].bitcast(I32), in_=w2_words[0].bitcast(I32))
         nc.gpsimd.dma_start(out=w23_raw[:, 2 * COLS : 4 * COLS].bitcast(I32), in_=w3_words[0].bitcast(I32))
+        gn_sb = load_column("gn_sb", gn)
         gk_sb = load_column("gk_sb", gk)
         n5_sb = load_list("n5_sb", n5)
         n6_sb = load_list("n6_sb", n6)
@@ -210,13 +212,12 @@ def tile_picked_jkeyoverknormedb_none_po_kernel(
 
         old, sg = [], []
         for t in range(PACK):
-            sg_t = sbuf("sg%d" % t, COLS + SCATTERED, F32)
-            nc.vector.tensor_copy(sg_t[:, COLS:], ds[t][:].indirect(n3_sb[:]))
+            sg_t = sbuf("sg%d" % t, COLS + SCATTERED, F32, "den3" if t == PACK - 1 else None)
+            if t < PACK - 1:
+                nc.vector.tensor_copy(sg_t[:, COLS:], ds[t][:].indirect(n3_sb[:]))
             old.append(sg_t[:, COLS:])
             sg.append(sg_t)
 
-        half_tile = sbuf("half_tile", 1, F32)
-        nc.vector.memset(half_tile[:], 0.5)
         for t in range(PACK):
             nc.scalar.activation(size[t][:, :COLS], size[t][:, COLS:], ACT.Ln, bias=half_tile[:])
 
@@ -231,10 +232,11 @@ def tile_picked_jkeyoverknormedb_none_po_kernel(
         for t in range(last):
             nc.vector.tensor_tensor(ds[t][:].indirect(n3_sb[:]), old[t], inv_den[t][:], ALU.mult)
             nc.vector.tensor_scalar(z2_rows[:, t, :], ds[t][:], gk_sb[:, t : t + 1], None, ALU.mult)
+        nc.scalar.activation(old[last], ds[last][:].indirect(n3_sb[:]), ACT.Copy)
         ratio = sbuf("ratio", SCATTERED, F32)
         nc.vector.tensor_tensor(ratio[:], old[last], inv_den[last][:], ALU.mult)
 
-        w23 = sbuf("w23", 4 * COLS, U8)
+        w23 = sbuf("w23", 4 * COLS, U8, "w1_raw")
         w3 = deal_fp4_words(w23[:, 2 * COLS : 4 * COLS], w23_raw[:, 2 * COLS : 4 * COLS])
         w2 = deal_fp4_words(w23[:, 0 : 2 * COLS], w23_raw[:, 0 : 2 * COLS])
         w23s = deal_scale_bytes("w23s", w23s_raw, 2)
@@ -271,21 +273,31 @@ def tile_picked_jkeyoverknormedb_none_po_kernel(
         for half, (start, stop) in enumerate(halves):
             grouped = interleave(nc.scalar.copy, "z2_grouped%d" % half, z2_rows, start, stop)
             z2_mx.append(quantize("z2_%d" % half, grouped, HALF))
-        for t in range(PACK):
-            accs = [bank("h_acc%d_%d" % (half, t), PACK * half + t, HALF) for half in range(2)]
+        bias = sbuf("bias", PACK, F32, "inv_den0")
+        nc.vector.scalar_tensor_tensor(bias[:], sl_sb[:], -1.0, th_sb[:], ALU.mult, ALU.mult)
+
+        def h_rows(t, copy):
+            accs = [bank("h_acc%d_%d" % (half, t), 2 * (t % 2) + half, HALF) for half in range(2)]
             for half in range(2):
                 fp4_pass(accs[half], w2, w23s, 0, t, *z_mx[half], True, False)
             for half, (start, stop) in enumerate(halves):
                 fp4_pass(accs[half], w3, w23s, COLS, t, *z2_mx[half], False, True)
-                nc.vector.tensor_copy(out=h[t][:, start:stop], in_=accs[half][:])
+                copy(out=h[t][:, start:stop], in_=accs[half][:])
 
-        bias = sbuf("bias", PACK, F32)
-        nc.vector.scalar_tensor_tensor(bias[:], sl_sb[:], -1.0, th_sb[:], ALU.mult, ALU.mult)
-        for t in range(PACK):
+        def gate(t):
             nc.scalar.activation(
                 sg[t][:, :COLS], h[t][:].indirect(n5_sb[:]), ACT.Sigmoid,
                 bias=bias[:, t : t + 1], scale=sl_sb[:, t : t + 1],
             )
+
+        h_rows(0, nc.vector.tensor_copy)
+        h_rows(1, nc.vector.tensor_copy)
+        gate(0)
+        h_rows(2, nc.vector.tensor_copy)
+        gate(1)
+        h_rows(3, nc.vector.tensor_copy)
+        gate(2)
+        gate(3)
 
         out_rows = out_0.rearrange("(p t) c -> p t c", t=PACK)
         out_words = out_1[0].rearrange("p c r -> p (c r)").bitcast(I32)
@@ -317,7 +329,7 @@ def tile_picked_jkeyoverknormedb_none_po_kernel(
             nc.vector.quantize_mx(
                 out=out_codes[:, start:stop].bitcast(FP8X4), scales=out_scales[:, start:stop], in_=grouped[half][:]
             )
-        nc.sync.dma_start(out=out_words, in_=out_codes[:].bitcast(I32))
+            nc.sync.dma_start(out=out_words[:, start:stop], in_=out_codes[:, start:stop].bitcast(I32))
         for q in range(QUADS):
             nc.sync.dma_start(
                 out=out_2[0, 4 * q : 4 * q + 4, :].bitcast(I32),

@@ -115,6 +115,9 @@ def tile_picked_jkeyoverknormedb_none_po_kernel(
         minus_one = sbuf("minus_one", 1, F32)
         nc.vector.memset(minus_one[:], -1.0)
 
+        warm = sbuf("warm", 1, F32)
+        nc.scalar.activation(warm[:], half_tile[:], ACT.Ln)
+
         offs_sb = load_list("offs_sb", offs)
         xw_table = sbuf("xw_table", TOKENS, I32)
         nc.sync.dma_start(out=xw_table[:], in_=x_words[0].rearrange("p n t -> p (n t)").bitcast(I32))

from contextlib import ExitStack

import concourse.mybir as mybir

F32 = mybir.dt.float32
BF16 = mybir.dt.bfloat16
I32 = mybir.dt.int32
U32 = mybir.dt.uint32
U16 = mybir.dt.uint16
U8 = mybir.dt.uint8
FP8X4 = mybir.dt.float8_e4m3fn_x4
FP4X4 = mybir.dt.float4_e2m1fn_x4
ACT = mybir.ActivationFunctionType
ALU = mybir.AluOpType

P = 128
PACK = 4
QUADS = 4
COLS = 512
HALF = COLS // 2
TOKENS = 1024
CODEWORDS = 2048
SCATTERED = 384
PER_COLUMN = 16
ODD_RUN_SHIFT = 14

PAD = 16

FLOPS = 4 * 2 * 512 * 512 * 512


def tile_picked_jkeyoverknormedb_none_po_kernel(
    tc, x_words, x_scales, w1_words, w1_scales, d_words, d_scales, gn, gk,
    w2_words, w2_scales, w3_words, w3_scales, sl, th,
    offs, kidx, two, n1, n2, n3, n4, n5, n6, out_0, out_1, out_2,
):
    nc = tc.nc
    with ExitStack() as ctx:
        sb = ctx.enter_context(tc.tile_pool(name="sb", bufs=1))
        ps = ctx.enter_context(tc.psum_pool(name="ps", bufs=1))

        def sbuf(name, width, dtype, tag=None):
            return sb.tile([P, width], dtype, name=name, tag=tag or name, align_bytes=64)

        def bank(name, number, width):
            return ps.tile([P, width], F32, name=name, tag="bank%d" % number)

        def load_list(name, src):
            dst = sb.tile([P, src.shape[1]], U16, name=name, tag=name)
            nc.sync.dma_start(dst[:], src)
            return dst

        def load_column(name, src):
            dst = sbuf(name, PACK, F32)
            nc.gpsimd.dma_start(out=dst[:], in_=src.rearrange("(p t) one -> p (t one)", t=PACK))
            return dst

        def load_scale_rows(dst, src, first):
            for q in range(QUADS):
                nc.sync.dma_start(
                    out=dst[32 * q + first : 32 * q + first + 4, :].bitcast(I32),
                    in_=src[0, 4 * q : 4 * q + 4, :].bitcast(I32),
                )

        def zeroed_plane(name, width, tag=None):
            plane = sbuf(name, width, U8, tag)
            nc.vector.memset(plane[:].bitcast(I32), 0)
            return plane

        def load_fp4_words(name, src, tag=None):
            dst = sbuf(name, 2 * COLS, U8, tag)
            nc.sync.dma_start(out=dst[:].bitcast(I32), in_=src[0].bitcast(I32))
            return dst

        def deal_fp4_words(dealt, raw):
            nc.scalar.copy(
                out=dealt[:].bitcast(U16).rearrange("p (t m) -> p t m", t=PACK),
                in_=raw[:].bitcast(U16).rearrange("p (m t) -> p t m", t=PACK),
            )
            return dealt

        def deal_scale_bytes(name, raw, count):
            dealt = sbuf(name, count * COLS, U8)
            nc.vector.tensor_copy(
                out=dealt[:].rearrange("p (w t m) -> p w t m", w=count, t=PACK),
                in_=raw[:].rearrange("p (w m t) -> p w t m", w=count, t=PACK),
            )
            return dealt

        def entries(offsets, start, stop):
            return offsets[:, start // PER_COLUMN : stop // PER_COLUMN]

        def interleave(copy, name, rows, start, stop, tag=None):
            grouped = sbuf(name, PACK * (stop - start), BF16, tag)
            copy(
                out=grouped[:].rearrange("p (c i t) -> p c t i", i=4, t=PACK),
                in_=rows[:, :, start:stop].rearrange("p t (c i) -> p c t i", i=4),
            )
            return grouped

        def quantize(name, grouped, width):
            codes = sbuf(name + "_codes", width, U32)
            scales = sbuf(name + "_scales", width, U8)
            nc.vector.quantize_mx(out=codes[:].bitcast(FP8X4), scales=scales[:], in_=grouped[:])
            return codes, scales

        halves = [(0, HALF), (HALF, COLS)]

        xs_table = zeroed_plane("xs_table", TOKENS)
        w1s_raw = zeroed_plane("w1s_raw", COLS)
        ds_table = zeroed_plane("ds_table", CODEWORDS)
        key_scales = zeroed_plane("key_scales", COLS)
        half_tile = sbuf("half_tile", 1, F32)
        nc.vector.memset(half_tile[:], 0.5)
        minus_one = sbuf("minus_one", 1, F32)
        nc.vector.memset(minus_one[:], -1.0)

        warm = sbuf("warm", 1, F32)
        nc.scalar.activation(warm[:], half_tile[:], ACT.Ln)

        offs_sb = load_list("offs_sb", offs)
        xw_table = sbuf("xw_table", TOKENS, I32)
        nc.sync.dma_start(out=xw_table[:], in_=x_words[0].rearrange("p n t -> p (n t)").bitcast(I32))
        load_scale_rows(xs_table, x_scales, 0)
        w1_raw = load_fp4_words("w1_raw", w1_words)
        kidx_sb = load_list("kidx_sb", kidx)
        load_scale_rows(w1s_raw, w1_scales, 0)
        load_scale_rows(ds_table, d_scales, ODD_RUN_SHIFT)
        two_sb = load_list("two_sb", two)
        n1_sb = load_list("n1_sb", n1)
        n2_sb = load_list("n2_sb", n2)
        n3_sb = load_list("n3_sb", n3)
        dw_table = sbuf("dw_table", CODEWORDS, I32)
        nc.sync.dma_start(out=dw_table[:], in_=d_words[0].rearrange("p n t -> p (n t)").bitcast(I32))
        n4_sb = load_list("n4_sb", n4)
        w23_raw = sbuf("w23_raw", 4 * COLS, U8)
        nc.gpsimd.dma_start(out=w23_raw[:, 0 : 2 * COLS].bitcast(I32), in_=w2_words[0].bitcast(I32))
        nc.gpsimd.dma_start(out=w23_raw[:, 2 * COLS : 4 * COLS].bitcast(I32), in_=w3_words[0].bitcast(I32))
        gn_sb = load_column("gn_sb", gn)
        gk_sb = load_column("gk_sb", gk)
        n5_sb = load_list("n5_sb", n5)
        n6_sb = load_list("n6_sb", n6)
        sl_sb = load_column("sl_sb", sl)
        th_sb = load_column("th_sb", th)

        w1 = deal_fp4_words(sbuf("w1", 2 * COLS, U8), w1_raw)
        w1s = deal_scale_bytes("w1s", w1s_raw, 1)
        xq_codes = sbuf("xq_codes", COLS, U32)
        nc.vector.tensor_copy(xq_codes[:], xw_table[:].bitcast(U32).indirect(offs_sb[:]))
        xq_scales = sbuf("xq_scales", COLS, U8)
        nc.vector.tensor_copy(xq_scales[:], xs_table[:].indirect(offs_sb[:]))

        def fp4_pass(acc, words, scales, first, t, codes, code_scales, start, stop):
            nc.tensor.matmul_mx(
                out=acc[:],
                lhsT=words[:, 2 * P * t : 2 * P * (t + 1)].bitcast(FP4X4),
                lhsT_scale=scales[:, first + P * t : first + P * (t + 1)],
                rhs=codes[:].bitcast(FP8X4),
                rhs_scale=code_scales[:],
                start=start,
                stop=stop,
            )

        y = []
        for t in range(PACK):
            acc = bank("y_acc%d" % t, t, COLS)
            fp4_pass(acc, w1, w1s, 0, t, xq_codes, xq_scales, True, True)
            y_t = sbuf("y%d" % t, COLS + PAD, F32)
            nc.vector.memset(y_t[:, COLS:], 0.0)
            nc.scalar.copy(out=y_t[:, :COLS], in_=acc[:])
            y.append(y_t)

        key_scales_picked = sbuf("key_scales_picked", COLS, U8, "late_scales")
        nc.vector.tensor_copy(key_scales_picked[:], ds_table[:].indirect(kidx_sb[:]))
        key_scales_dealt = deal_scale_bytes("key_scales_dealt", key_scales_picked, 1)
        for q in range(QUADS):
            nc.sync.dma_start(
                out=key_scales[32 * q : 32 * q + 4, :].bitcast(I32),
                in_=key_scales_dealt[32 * q + ODD_RUN_SHIFT : 32 * q + ODD_RUN_SHIFT + 4, :].bitcast(I32),
            )
        x2_codes = sbuf("x2_codes", COLS, U32)
        nc.vector.tensor_copy(x2_codes[:], xw_table[:].bitcast(U32).indirect(two_sb[:]))
        x2_scales = sbuf("x2_scales", COLS, U8)
        nc.vector.tensor_copy(x2_scales[:], xs_table[:].indirect(two_sb[:]))
        key_codes_picked = sbuf("key_codes_picked", COLS, U32)
        nc.vector.tensor_copy(key_codes_picked[:], dw_table[:].bitcast(U32).indirect(kidx_sb[:]))
        key_codes = sbuf("key_codes", COLS, U32)
        nc.vector.tensor_copy(
            out=key_codes[:].rearrange("p (t m) -> p m t", t=PACK),
            in_=key_codes_picked[:].rearrange("p (m t) -> p m t", t=PACK),
        )

        w23s_raw = zeroed_plane("w23s_raw", 2 * COLS, "late_scales")
        load_scale_rows(w23s_raw[:, 0:COLS], w2_scales, 0)
        load_scale_rows(w23s_raw[:, COLS : 2 * COLS], w3_scales, 0)

        ds, size = [], []
        for t in range(PACK):
            acc = bank("s_acc%d" % t, PACK + t, COLS)
            nc.tensor.matmul_mx(
                out=acc[:],
                lhsT=key_codes[:, P * t : P * (t + 1)].bitcast(FP8X4),
                lhsT_scale=key_scales[:, P * t : P * (t + 1)],
                rhs=x2_codes[:].bitcast(FP8X4),
                rhs_scale=x2_scales[:],
                start=True,
                stop=True,
            )
            size_t = sbuf("den%d" % t, 2 * COLS, F32)
            nc.scalar.activation(size_t[:, COLS:], acc[:], ACT.Abs, scale=0.0625)
            ds_t = sbuf("ds%d" % t, COLS, F32)
            nc.vector.tensor_scalar(ds_t[:], acc[:], 0.0625, None, ALU.mult)
            size.append(size_t)
            ds.append(ds_t)

        old, sg = [], []
        for t in range(PACK):
            sg_t = sbuf("sg%d" % t, COLS + SCATTERED, F32, "den3" if t == PACK - 1 else None)
            if t < PACK - 1:
                nc.vector.tensor_copy(sg_t[:, COLS:], ds[t][:].indirect(n3_sb[:]))
            old.append(sg_t[:, COLS:])
            sg.append(sg_t)

        for t in range(PACK):
            nc.scalar.activation(size[t][:, :COLS], size[t][:, COLS:], ACT.Ln, bias=half_tile[:])

        inv_den = []
        for t in range(PACK):
            inv_t = sbuf("inv_den%d" % t, SCATTERED, F32)
            nc.scalar.activation(inv_t[:], size[t][:].indirect(n4_sb[:]), ACT.Exp, scale=minus_one[:])
            inv_den.append(inv_t)

        z2_rows = sb.tile([P, PACK, COLS], BF16, name="z2_rows", align_bytes=64)
        last = PACK - 1
        for t in range(last):
            nc.vector.tensor_tensor(ds[t][:].indirect(n3_sb[:]), old[t], inv_den[t][:], ALU.mult)
            nc.vector.tensor_scalar(z2_rows[:, t, :], ds[t][:], gk_sb[:, t : t + 1], None, ALU.mult)
        nc.scalar.activation(old[last], ds[last][:].indirect(n3_sb[:]), ACT.Copy)
        ratio = sbuf("ratio", SCATTERED, F32)
        nc.vector.tensor_tensor(ratio[:], old[last], inv_den[last][:], ALU.mult)

        w23 = sbuf("w23", 4 * COLS, U8, "w1_raw")
        w3 = deal_fp4_words(w23[:, 2 * COLS : 4 * COLS], w23_raw[:, 2 * COLS : 4 * COLS])
        w2 = deal_fp4_words(w23[:, 0 : 2 * COLS], w23_raw[:, 0 : 2 * COLS])
        w23s = deal_scale_bytes("w23s", w23s_raw, 2)

        y_terms = sb.tile([P, 2 * PACK, COLS], F32, name="y_terms", tag="key_codes_picked", align_bytes=64)
        for t in range(PACK):
            nc.vector.tensor_scalar(y_terms[:, t, :], y[t][:, :COLS], gn_sb[:, t : t + 1], -0.75, ALU.mult, ALU.mult)

        h = [sbuf("h%d" % t, 2 * COLS, F32, (None, None, "den1", "den2")[t]) for t in range(PACK)]
        second_early = sbuf("second_early", COLS, F32)
        second_late = sb.tile([P, PACK - 1, COLS], F32, name="second_late", tag="den0", align_bytes=64)
        z_rows = sb.tile([P, PACK, COLS], BF16, name="z_rows", align_bytes=64)

        def z_piece(t, start, stop):
            first = h[t][:, COLS + start : COLS + stop]
            second = second_early[:, start:stop] if t == 0 else second_late[:, t - 1, start:stop]
            larger = y_terms[:, PACK + t, start:stop]
            nc.scalar.activation(first, y[t][:].indirect(entries(n1_sb, start, stop)), ACT.Copy)
            nc.scalar.activation(second, y[t][:].indirect(entries(n2_sb, start, stop)), ACT.Copy)
            nc.vector.tensor_tensor(larger, first, second, ALU.max)
            nc.vector.scalar_tensor_tensor(
                z_rows[:, t, start:stop], larger, gn_sb[:, t : t + 1], y_terms[:, t, start:stop], ALU.mult, ALU.add
            )

        for t in range(PACK):
            z_piece(t, 0, COLS)
        nc.scalar.activation(ds[last][:].indirect(n3_sb[:]), ratio[:], ACT.Copy)
        nc.scalar.activation(z2_rows[:, last, :], ds[last][:], ACT.Copy, scale=gk_sb[:, last : last + 1])

        z_mx, z2_mx = [], []
        for half, (start, stop) in enumerate(halves):
            grouped = interleave(nc.vector.tensor_copy, "z_grouped%d" % half, z_rows, start, stop)
            z_mx.append(quantize("z_%d" % half, grouped, HALF))
        for half, (start, stop) in enumerate(halves):
            grouped = interleave(nc.scalar.copy, "z2_grouped%d" % half, z2_rows, start, stop)
            z2_mx.append(quantize("z2_%d" % half, grouped, HALF))
        bias = sbuf("bias", PACK, F32, "inv_den0")
        nc.vector.scalar_tensor_tensor(bias[:], sl_sb[:], -1.0, th_sb[:], ALU.mult, ALU.mult)

        def h_rows(t, copy):
            accs = [bank("h_acc%d_%d" % (half, t), 2 * (t % 2) + half, HALF) for half in range(2)]
            for half in range(2):
                fp4_pass(accs[half], w2, w23s, 0, t, *z_mx[half], True, False)
            for half, (start, stop) in enumerate(halves):
                fp4_pass(accs[half], w3, w23s, COLS, t, *z2_mx[half], False, True)
                copy(out=h[t][:, start:stop], in_=accs[half][:])

        def gate(t):
            nc.scalar.activation(
                sg[t][:, :COLS], h[t][:].indirect(n5_sb[:]), ACT.Sigmoid,
                bias=bias[:, t : t + 1], scale=sl_sb[:, t : t + 1],
            )

        h_rows(0, nc.vector.tensor_copy)
        h_rows(1, nc.vector.tensor_copy)
        gate(0)
        h_rows(2, nc.vector.tensor_copy)
        gate(1)
        h_rows(3, nc.vector.tensor_copy)
        gate(2)
        gate(3)

        out_rows = out_0.rearrange("(p t) c -> p t c", t=PACK)
        out_words = out_1[0].rearrange("p c r -> p (c r)").bitcast(I32)
        result = sb.tile([P, PACK, COLS], F32, name="result", align_bytes=64)

        def out_piece(t, start, stop):
            label = "%d_%d" % (t, start)
            other = sbuf("other" + label, stop - start, F32)
            looked_up = sg[t][:].indirect(entries(n6_sb, start, stop))
            if t < 2:
                nc.vector.tensor_copy(other[:], looked_up)
            else:
                nc.scalar.activation(other[:], looked_up, ACT.Copy)
            gap = sbuf("gap" + label, stop - start, F32)
            nc.vector.tensor_tensor(gap[:], sg[t][:, start:stop], other[:], ALU.subtract)
            nc.vector.scalar_tensor_tensor(result[:, t, start:stop], gap[:], 1.5, h[t][:, start:stop], ALU.mult, ALU.mult)
            nc.sync.dma_start(out=out_rows[:, t, start:stop], in_=result[:, t, start:stop])

        for t in range(PACK - 1):
            out_piece(t, 0, COLS)
        out_codes = sbuf("out_codes", COLS, U32)
        out_scales = sbuf("out_scales", COLS, U8)
        grouped = []
        for half, (start, stop) in enumerate(halves):
            out_piece(PACK - 1, start, stop)
            copy = nc.scalar.copy if half == 0 else nc.vector.tensor_copy
            grouped.append(interleave(copy, "out_grouped%d" % half, result, start, stop))
        for half, (start, stop) in enumerate(halves):
            nc.vector.quantize_mx(
                out=out_codes[:, start:stop].bitcast(FP8X4), scales=out_scales[:, start:stop], in_=grouped[half][:]
            )
            nc.sync.dma_start(out=out_words[:, start:stop], in_=out_codes[:, start:stop].bitcast(I32))
        for q in range(QUADS):
            nc.sync.dma_start(
                out=out_2[0, 4 * q : 4 * q + 4, :].bitcast(I32),
                in_=out_scales[32 * q : 32 * q + 4, :].bitcast(I32),
            )
